import numpy as np
import ml_dtypes


def mxq(x, axis, fmt="e4m3"):
    dtype, down = {"e4m3": (ml_dtypes.float8_e4m3fn, 7), "e5m2": (ml_dtypes.float8_e5m2, 14)}[fmt]
    v = np.moveaxis(np.asarray(x, np.float32).astype(ml_dtypes.bfloat16).astype(np.float64), axis, -1)
    blocks = v.reshape(v.shape[:-1] + (-1, 32))
    amax = np.abs(blocks).max(-1, keepdims=True)
    byte = np.maximum(np.where(amax > 0, np.frexp(amax)[1] - 1 + 127, 0) - down, 1)
    scale = np.exp2(byte - 127.0)
    codes = (blocks / scale).astype(np.float32).astype(dtype).astype(np.float64)
    return np.moveaxis((codes * scale).reshape(v.shape), -1, axis)


WIDE = False


def mx_kscale(k):
    if not WIDE:
        return np.ones(k)
    levels = np.array([10, -10, 5, -5, 0])
    if k % 512:
        return np.exp2(np.random.permutation(np.resize(levels, k // 32))).repeat(32)
    a = np.empty((k // 512, 16))
    for p in range(k // 512):
        a[p, :8] = np.random.permutation(np.resize(levels, 8))
        for g in range(8):
            far = levels[np.abs(levels - a[p, g]) >= 10]
            a[p, g + 8] = far[np.random.randint(len(far))]
    return np.exp2(a.ravel()).repeat(32)


def f64(x):
    return np.asarray(x).astype(np.float64)


def striped(idx):
    return np.tile(idx.reshape(-1, 16).T, (8, 1)).astype(np.uint16)


def unstriped(offs):
    return offs[:16].T.reshape(-1).astype(np.int64)


def gelu(v):
    return 0.5 * v * (1.0 + np.tanh(np.sqrt(2.0 / np.pi) * (v + 0.044715 * v**3)))


K, T, S, V, H, N = 512, 2048, 1024, 2048, 1024, 128
P = 2 ** 7


def setup_inputs():
    n = np.random.standard_normal
    s = mx_kscale(K)[:, None]
    u = mx_kscale(H)
    return {
        "xT": (n((K, T)) * s).astype(np.float32),
        "w1": (n((K, H)) / np.sqrt(K) / s * u).astype(np.float32),
        "w2": (n((H, N)) / np.sqrt(H) / u[:, None]).astype(np.float32),
        "gate": np.tile(np.random.uniform(0.5, 1.5, S), (P, 1)).astype(np.float32),
        "offs": striped(np.random.permutation(T)[:S]),
        "pos1": striped(np.random.permutation(V)[:S]),
    }


def reference(xT, w1, w2, gate, offs, pos1):
    h = gelu(mxq(f64(w1), 0, "e4m3").T @ mxq(f64(xT)[:, unstriped(offs)], 0, "e4m3"))
    z = np.zeros((H, V))
    z[:, unstriped(pos1)] = f64(gate)[:1] * h
    return mxq(f64(w2), 0, "e4m3").T @ mxq(z, 0, "e4m3")

@@ -1,0 +1,202 @@
+from contextlib import ExitStack
+
+import concourse.mybir as mybir
+
+K, T, S, V, H, N = 512, 2048, 1024, 2048, 1024, 128
+FLOPS = 2 * K * H * S + 2 * H * N * V
+
+F32 = mybir.dt.float32
+BF16 = mybir.dt.bfloat16
+I32 = mybir.dt.int32
+U32 = mybir.dt.uint32
+U16 = mybir.dt.uint16
+U8 = mybir.dt.uint8
+FP8X4 = mybir.dt.float8_e4m3fn_x4
+GELU = mybir.ActivationFunctionType.Gelu_apprx_tanh
+MULT = mybir.AluOpType.mult
+
+P = 128
+PACK = 4
+KP = P * PACK
+BANK = 512
+X_CHUNKS = [512, 512, 512, 256, 256]
+
+
+def tile_picked_voxel_gelu_e_kernel(tc, xT, w1, w2, gate, offs, pos1, out):
+    nc = tc.nc
+    with ExitStack() as ctx:
+        keep = ctx.enter_context(tc.tile_pool(name="keep", bufs=1))
+        psum = ctx.enter_context(tc.psum_pool(name="psum", bufs=1))
+
+        offs_sb = keep.tile([P, S // 16], U16, name="offs_sb")
+        pos_sb = keep.tile([P, S // 16], U16, name="pos_sb")
+        x_raw = [keep.tile([P, PACK, w], F32, name="x_raw%d" % i, tag="big%d" % i, align_bytes=64) for i, w in enumerate(X_CHUNKS)]
+        x_bf = [keep.tile([P, w, PACK], BF16, name="x_bf%d" % i, align_bytes=64) for i, w in enumerate(X_CHUNKS)]
+        x_codes = keep.tile([P, T], U32, name="x_codes", align_bytes=64)
+        x_scales = keep.tile([P, T], U8, name="x_scales", align_bytes=64)
+        g_codes = keep.tile([P, S], U32, name="g_codes", align_bytes=64)
+        g_scales = keep.tile([P, S], U8, name="g_scales", align_bytes=64)
+        w1_raw = [keep.tile([P, PACK, KP // 2], F32, name="w1_raw%d" % i, align_bytes=64) for i in range(4)]
+        w1_bf = [keep.tile([P, PACK, P, PACK], BF16, name="w1_bf%d" % c, align_bytes=64) for c in range(2)]
+        w1_codes = keep.tile([P, H], U32, name="w1_codes", align_bytes=64)
+        w1_scales = keep.tile([P, H], U8, name="w1_scales", align_bytes=64)
+        w2_raw = keep.tile([P, 2, PACK, N], F32, name="w2_raw", align_bytes=64)
+        w2_bf = keep.tile([P, 2, N, PACK], BF16, name="w2_bf", align_bytes=64)
+        w2_codes = keep.tile([P, 2 * N], U32, name="w2_codes", align_bytes=64)
+        w2_scales = keep.tile([P, 2 * N], U8, name="w2_scales", align_bytes=64)
+        gate_sb = keep.tile([P, S], F32, name="gate_sb", align_bytes=64)
+        h_sb = {}
+        cells = [keep.tile([P, V], F32, name="cells%d" % t, align_bytes=64) for t in range(PACK)]
+        pairs = keep.tile([P, 2, V, 2], BF16, name="pairs", align_bytes=64)
+        z_bf = [keep.tile([P, V, PACK], BF16, name="z_bf%d" % c, align_bytes=64) for c in range(2)]
+        z_codes = keep.tile([P, 2, V], U32, name="z_codes", align_bytes=64)
+        z_scales = keep.tile([P, 2, V], U8, name="z_scales", align_bytes=64)
+        warm = keep.tile([P, 8], F32, name="warm")
+        out_ps = [psum.tile([P, BANK], F32, name="out_ps%d" % q) for q in range(4)]
+
+        xv = xT.rearrange("(p j) w -> p j w", j=PACK)
+        w1v = w1.rearrange("(p j) c -> p j c", j=PACK)
+        starts = [sum(X_CHUNKS[:i]) for i in range(len(X_CHUNKS))]
+        for i, w in enumerate(X_CHUNKS):
+            if i == len(X_CHUNKS) - 1:
+                nc.sync.dma_start(offs_sb[:], offs)
+            nc.sync.dma_start(out=x_raw[i][:], in_=xv[:, :, starts[i]:starts[i] + w])
+        for i in range(2):
+            nc.sync.dma_start(out=w1_raw[i][:], in_=w1v[:, :, i * 256:(i + 1) * 256])
+        nc.sync.dma_start(pos_sb[:], pos1)
+        nc.sync.dma_start(out=gate_sb[:], in_=gate)
+        for i in range(2, 4):
+            nc.sync.dma_start(out=w1_raw[i][:], in_=w1v[:, :, i * 256:(i + 1) * 256])
+        for c in range(2):
+            nc.sync.dma_start(out=w2_raw[:, c, :, :], in_=w2[c * KP:(c + 1) * KP, :].rearrange("(p j) n -> p j n", j=PACK))
+
+        nc.vector.memset(warm[:, 0:1], 0.0)
+        nc.scalar.activation(out=warm[:, 4:5], in_=warm[:, 0:1], func=GELU)
+        nc.vector.memset(x_scales[:].bitcast(I32), 0)
+        for t in range(PACK):
+            nc.vector.memset(cells[t][:], 0.0)
+
+        def quantize(codes, scales, src):
+            nc.vector.quantize_mx(out=codes.bitcast(FP8X4), scales=scales, in_=src)
+
+        def interleave(engine_copy, dst, src):
+            engine_copy(out=dst.rearrange("p (c i) t -> p c t i", i=4), in_=src.rearrange("p t (c i) -> p c t i", i=4))
+
+        for i, w in enumerate(X_CHUNKS):
+            cut = w * 3 // 8
+            interleave(nc.scalar.copy, x_bf[i][:, 0:cut, :], x_raw[i][:, :, 0:cut])
+            interleave(nc.vector.tensor_copy, x_bf[i][:, cut:w, :], x_raw[i][:, :, cut:w])
+            cols = slice(starts[i], starts[i] + w)
+            quantize(x_codes[:, cols], x_scales[:, cols], x_bf[i][:].rearrange("p w t -> p (w t)"))
+
+        def w1_copy(c):
+            for half in range(2):
+                nc.scalar.copy(
+                    out=w1_bf[c][:, :, half * 64:(half + 1) * 64, :].rearrange("p t m j -> p m j t"),
+                    in_=w1_raw[2 * c + half][:].rearrange("p j (m t) -> p m j t", t=PACK),
+                )
+
+        def w1_quantize(c):
+            cols = slice(c * KP, (c + 1) * KP)
+            quantize(w1_codes[:, cols], w1_scales[:, cols], w1_bf[c][:].rearrange("p t m j -> p (t m j)"))
+
+        def gather(half):
+            cols = slice(half * BANK, (half + 1) * BANK)
+            lst = offs_sb[:, half * 32:(half + 1) * 32]
+            nc.vector.tensor_copy(g_codes[:, cols], x_codes[:].indirect(lst))
+            nc.vector.tensor_copy(g_scales[:, cols], x_scales[:].indirect(lst))
+
+        def layer1(n, half):
+            cols = slice(half * BANK, (half + 1) * BANK)
+            wc = slice(n * P, (n + 1) * P)
+            if half == 0:
+                h_sb.setdefault(n, keep.tile([P, S], F32, name="h_sb", bufs=5, align_bytes=64))
+            acc = psum.tile([P, BANK], F32, name="h_ps", bufs=4)
+            nc.tensor.matmul_mx(
+                out=acc[:], lhsT=w1_codes[:, wc].bitcast(FP8X4), lhsT_scale=w1_scales[:, wc],
+                rhs=g_codes[:, cols].bitcast(FP8X4), rhs_scale=g_scales[:, cols], start=True, stop=True,
+            )
+            nc.scalar.activation(out=h_sb[n][:, cols], in_=acc[:], func=GELU)
+
+        def scatter(n, a, b):
+            nc.vector.tensor_tensor(
+                cells[n % PACK][:].indirect(pos_sb[:, a // 16:b // 16]), h_sb[n][:, a:b], gate_sb[:, a:b], MULT)
+
+        def layer2(c, q):
+            cols = slice(q * BANK, (q + 1) * BANK)
+            wc = slice(c * N, (c + 1) * N)
+            nc.tensor.matmul_mx(
+                out=out_ps[q][:], lhsT=w2_codes[:, wc].bitcast(FP8X4), lhsT_scale=w2_scales[:, wc],
+                rhs=z_codes[:, c, cols].bitcast(FP8X4), rhs_scale=z_scales[:, c, cols], start=(c == 0), stop=(c == 1),
+            )
+
+        def z_quantize(c, a, b):
+            quantize(z_codes[:, c, a:b], z_scales[:, c, a:b], z_bf[c][:, a:b, :].rearrange("p v t -> p (v t)"))
+
+        def to_pairs(t):
+            nc.scalar.copy(out=pairs[:, t // 2, :, t % 2], in_=cells[t][:])
+
+        w1_copy(0)
+        gather(0)
+        w1_quantize(0)
+        gather(1)
+        layer1(0, 0)
+        layer1(0, 1)
+        layer1(1, 0)
+        layer1(1, 1)
+        w1_copy(1)
+        scatter(0, 0, BANK)
+        scatter(0, BANK, S)
+        w1_quantize(1)
+        for n in (2, 3):
+            layer1(n, 0)
+            layer1(n, 1)
+        scatter(1, 0, S)
+        to_pairs(0)
+        for c in range(2):
+            interleave(nc.scalar.copy, w2_bf[:, c, :, :], w2_raw[:, c, :, :])
+        for n in (4, 5):
+            layer1(n, 0)
+            layer1(n, 1)
+        scatter(2, 0, S)
+        to_pairs(1)
+        for n in (6, 7):
+            layer1(n, 0)
+            layer1(n, 1)
+        scatter(3, 0, S)
+        quantize(w2_codes[:], w2_scales[:], w2_bf[:].rearrange("p c n j -> p (c n j)"))
+        to_pairs(2)
+        scatter(4, 0, S)
+        to_pairs(3)
+        words = pairs[:].rearrange("p u v e -> p u (v e)").bitcast(F32)
+        z0_words = z_bf[0][:].rearrange("p v t -> p (v t)").bitcast(F32).rearrange("p (v u) -> p v u", u=2)
+        interleave(nc.scalar.copy, z0_words, words)
+        scatter(5, 0, S)
+        nc.scalar.copy(out=z_bf[1][:, :, 0], in_=cells[0][:])
+        scatter(6, 0, S)
+        nc.scalar.copy(out=z_bf[1][:, :, 1], in_=cells[1][:])
+        z_quantize(0, 0, V // 2)
+        z_quantize(0, V // 2, V)
+        for q in range(4):
+            layer2(0, q)
+        scatter(7, 0, S)
+        half = V // 2
+        nc.scalar.copy(out=z_bf[1][:, 0:half, 2:4], in_=cells[2][:, 0:half].unsqueeze(2).to_broadcast([P, half, 2]))
+        nc.scalar.copy(out=z_bf[1][:, half:V, 2], in_=cells[2][:, half:V])
+        for q in (0, 1):
+            cols = slice(q * BANK, (q + 1) * BANK)
+            nc.vector.tensor_copy(out=z_bf[1][:, cols, 3], in_=cells[3][:, cols])
+        for q in (2, 3):
+            cols = slice(q * BANK, (q + 1) * BANK)
+            nc.scalar.copy(out=z_bf[1][:, cols, 3], in_=cells[3][:, cols])
+        for q in range(4):
+            z_quantize(1, q * BANK, (q + 1) * BANK)
+            layer2(1, q)
+        out_sb = keep.tile([P, V], F32, name="out_sb", tag="big0", align_bytes=64)
+        for q in range(4):
+            cols = slice(q * BANK, (q + 1) * BANK)
+            if q == 2:
+                nc.vector.tensor_copy(out=out_sb[:, cols], in_=out_ps[q][:])
+            else:
+                nc.scalar.copy(out=out_sb[:, cols], in_=out_ps[q][:])
+            nc.sync.dma_start(out=out[:, cols], in_=out_sb[:, cols])

@@ -32,11 +32,12 @@ def tile_picked_voxel_gelu_e_kernel(tc, xT, w1, w2, gate, offs, pos1, out):
         pos_sb = keep.tile([P, S // 16], U16, name="pos_sb")
         x_raw = [keep.tile([P, PACK, w], F32, name="x_raw%d" % i, tag="big%d" % i, align_bytes=64) for i, w in enumerate(X_CHUNKS)]
         x_bf = [keep.tile([P, w, PACK], BF16, name="x_bf%d" % i, align_bytes=64) for i, w in enumerate(X_CHUNKS)]
-        x_codes = keep.tile([P, T], U32, name="x_codes", align_bytes=64)
-        x_scales = keep.tile([P, T], U8, name="x_scales", align_bytes=64)
+        x_codes = keep.tile([P, T], U32, name="x_codes", tag="later1", align_bytes=64)
+        x_scales = keep.tile([P, T], U8, name="x_scales", tag="later2", align_bytes=64)
         g_codes = keep.tile([P, S], U32, name="g_codes", align_bytes=64)
-        g_scales = keep.tile([P, S], U8, name="g_scales", align_bytes=64)
+        g_scales = [keep.tile([P, BANK], U8, name="g_scales0", align_bytes=64)]
         w1_raw = [keep.tile([P, PACK, KP // 2], F32, name="w1_raw%d" % i, align_bytes=64) for i in range(4)]
+        w1_first = keep.tile([P, P, PACK], BF16, name="w1_first", tag="later0", align_bytes=64)
         w1_bf = [keep.tile([P, PACK, P, PACK], BF16, name="w1_bf%d" % c, align_bytes=64) for c in range(2)]
         w1_codes = keep.tile([P, H], U32, name="w1_codes", align_bytes=64)
         w1_scales = keep.tile([P, H], U8, name="w1_scales", align_bytes=64)
@@ -46,9 +47,9 @@ def tile_picked_voxel_gelu_e_kernel(tc, xT, w1, w2, gate, offs, pos1, out):
         w2_scales = keep.tile([P, 2 * N], U8, name="w2_scales", align_bytes=64)
         gate_sb = keep.tile([P, S], F32, name="gate_sb", align_bytes=64)
         h_sb = {}
-        cells = [keep.tile([P, V], F32, name="cells%d" % t, align_bytes=64) for t in range(PACK)]
-        pairs = keep.tile([P, 2, V, 2], BF16, name="pairs", align_bytes=64)
-        z_bf = [keep.tile([P, V, PACK], BF16, name="z_bf%d" % c, align_bytes=64) for c in range(2)]
+        cells = [keep.tile([P, V], F32, name="cells0", align_bytes=64)]
+        pairs = keep.tile([P, 2, V, 2], BF16, name="pairs", tag="pairs", align_bytes=64)
+        z_bf = [keep.tile([P, V, PACK], BF16, name="z_bf0", align_bytes=64)]
         z_codes = keep.tile([P, 2, V], U32, name="z_codes", align_bytes=64)
         z_scales = keep.tile([P, 2, V], U8, name="z_scales", align_bytes=64)
         warm = keep.tile([P, 8], F32, name="warm")
@@ -73,8 +74,7 @@ def tile_picked_voxel_gelu_e_kernel(tc, xT, w1, w2, gate, offs, pos1, out):
         nc.vector.memset(warm[:, 0:1], 0.0)
         nc.scalar.activation(out=warm[:, 4:5], in_=warm[:, 0:1], func=GELU)
         nc.vector.memset(x_scales[:].bitcast(I32), 0)
-        for t in range(PACK):
-            nc.vector.memset(cells[t][:], 0.0)
+        nc.vector.memset(cells[0][:].bitcast(I32), 0)
 
         def quantize(codes, scales, src):
             nc.vector.quantize_mx(out=codes.bitcast(FP8X4), scales=scales, in_=src)
@@ -89,22 +89,28 @@ def tile_picked_voxel_gelu_e_kernel(tc, xT, w1, w2, gate, offs, pos1, out):
             cols = slice(starts[i], starts[i] + w)
             quantize(x_codes[:, cols], x_scales[:, cols], x_bf[i][:].rearrange("p w t -> p (w t)"))
 
-        def w1_copy(c):
+        def w1_copy(c, t0):
             for half in range(2):
                 nc.scalar.copy(
-                    out=w1_bf[c][:, :, half * 64:(half + 1) * 64, :].rearrange("p t m j -> p m j t"),
-                    in_=w1_raw[2 * c + half][:].rearrange("p j (m t) -> p m j t", t=PACK),
+                    out=w1_bf[c][:, t0:PACK, half * 64:(half + 1) * 64, :].rearrange("p t m j -> p m j t"),
+                    in_=w1_raw[2 * c + half][:].rearrange("p j (m t) -> p m j t", t=PACK)[:, :, :, t0:PACK],
                 )
 
-        def w1_quantize(c):
-            cols = slice(c * KP, (c + 1) * KP)
-            quantize(w1_codes[:, cols], w1_scales[:, cols], w1_bf[c][:].rearrange("p t m j -> p (t m j)"))
+        def w1_quantize(c, t0, t1):
+            cols = slice(c * KP + t0 * P, c * KP + t1 * P)
+            quantize(w1_codes[:, cols], w1_scales[:, cols], w1_bf[c][:, t0:t1, :, :].rearrange("p t m j -> p (t m j)"))
 
-        def gather(half):
-            cols = slice(half * BANK, (half + 1) * BANK)
+        def new_cells(t):
+            cells.append(keep.tile([P, V], F32, name="cells%d" % t, tag="later%d" % t, align_bytes=64))
+            nc.gpsimd.memset(cells[t][:], 0.0)
+
+        def gather_codes(half):
             lst = offs_sb[:, half * 32:(half + 1) * 32]
-            nc.vector.tensor_copy(g_codes[:, cols], x_codes[:].indirect(lst))
-            nc.vector.tensor_copy(g_scales[:, cols], x_scales[:].indirect(lst))
+            nc.vector.tensor_copy(g_codes[:, half * BANK:(half + 1) * BANK], x_codes[:].indirect(lst))
+
+        def gather_scales(half):
+            lst = offs_sb[:, half * 32:(half + 1) * 32]
+            nc.vector.tensor_copy(g_scales[half][:], x_scales[:].indirect(lst))
 
         def layer1(n, half):
             cols = slice(half * BANK, (half + 1) * BANK)
@@ -114,13 +120,18 @@ def tile_picked_voxel_gelu_e_kernel(tc, xT, w1, w2, gate, offs, pos1, out):
             acc = psum.tile([P, BANK], F32, name="h_ps", bufs=4)
             nc.tensor.matmul_mx(
                 out=acc[:], lhsT=w1_codes[:, wc].bitcast(FP8X4), lhsT_scale=w1_scales[:, wc],
-                rhs=g_codes[:, cols].bitcast(FP8X4), rhs_scale=g_scales[:, cols], start=True, stop=True,
+                rhs=g_codes[:, cols].bitcast(FP8X4), rhs_scale=g_scales[half][:], start=True, stop=True,
             )
             nc.scalar.activation(out=h_sb[n][:, cols], in_=acc[:], func=GELU)
 
         def scatter(n, a, b):
+            if n in (1, 2):
+                hg = keep.tile([P, S], F32, name="hg", bufs=2, align_bytes=64)
+                nc.vector.tensor_tensor(hg[:], h_sb[n][:], gate_sb[:], MULT)
+                nc.vector.tensor_copy(cells[n % 3][:].indirect(pos_sb[:]), hg[:])
+                return
             nc.vector.tensor_tensor(
-                cells[n % PACK][:].indirect(pos_sb[:, a // 16:b // 16]), h_sb[n][:, a:b], gate_sb[:, a:b], MULT)
+                cells[n % 3][:].indirect(pos_sb[:, a // 16:b // 16]), h_sb[n][:, a:b], gate_sb[:, a:b], MULT)
 
         def layer2(c, q):
             cols = slice(q * BANK, (q + 1) * BANK)
@@ -134,20 +145,32 @@ def tile_picked_voxel_gelu_e_kernel(tc, xT, w1, w2, gate, offs, pos1, out):
             quantize(z_codes[:, c, a:b], z_scales[:, c, a:b], z_bf[c][:, a:b, :].rearrange("p v t -> p (v t)"))
 
         def to_pairs(t):
-            nc.scalar.copy(out=pairs[:, t // 2, :, t % 2], in_=cells[t][:])
+            nc.scalar.copy(out=pairs[:, t // 2, :, t % 2], in_=cells[t % 3][:])
 
-        w1_copy(0)
-        gather(0)
-        w1_quantize(0)
-        gather(1)
+        for half in range(2):
+            nc.scalar.copy(
+                out=w1_first[:, half * 64:(half + 1) * 64, :],
+                in_=w1_raw[half][:].rearrange("p j (m t) -> p t m j", t=PACK)[:, 0, :, :],
+            )
+        w1_copy(0, 1)
+        gather_codes(0)
+        gather_scales(0)
+        gather_codes(1)
+        quantize(w1_codes[:, 0:P], w1_scales[:, 0:P], w1_first[:].rearrange("p m j -> p (m j)"))
+        g_scales.append(keep.tile([P, BANK], U8, name="g_scales1", tag="later0", align_bytes=64))
+        gather_scales(1)
+        w1_quantize(0, 1, 2)
+        w1_quantize(0, 2, 4)
+        new_cells(1)
+        new_cells(2)
         layer1(0, 0)
         layer1(0, 1)
         layer1(1, 0)
         layer1(1, 1)
-        w1_copy(1)
+        w1_copy(1, 0)
         scatter(0, 0, BANK)
         scatter(0, BANK, S)
-        w1_quantize(1)
+        w1_quantize(1, 0, 4)
         for n in (2, 3):
             layer1(n, 0)
             layer1(n, 1)
@@ -171,24 +194,25 @@ def tile_picked_voxel_gelu_e_kernel(tc, xT, w1, w2, gate, offs, pos1, out):
         words = pairs[:].rearrange("p u v e -> p u (v e)").bitcast(F32)
         z0_words = z_bf[0][:].rearrange("p v t -> p (v t)").bitcast(F32).rearrange("p (v u) -> p v u", u=2)
         interleave(nc.scalar.copy, z0_words, words)
+        z_bf.append(keep.tile([P, V, PACK], BF16, name="z_bf1", tag="pairs", align_bytes=64))
         scatter(5, 0, S)
-        nc.scalar.copy(out=z_bf[1][:, :, 0], in_=cells[0][:])
+        nc.scalar.copy(out=z_bf[1][:, :, 0], in_=cells[1][:])
         scatter(6, 0, S)
-        nc.scalar.copy(out=z_bf[1][:, :, 1], in_=cells[1][:])
+        nc.scalar.copy(out=z_bf[1][:, :, 1], in_=cells[2][:])
         z_quantize(0, 0, V // 2)
         z_quantize(0, V // 2, V)
         for q in range(4):
             layer2(0, q)
         scatter(7, 0, S)
         half = V // 2
-        nc.scalar.copy(out=z_bf[1][:, 0:half, 2:4], in_=cells[2][:, 0:half].unsqueeze(2).to_broadcast([P, half, 2]))
-        nc.scalar.copy(out=z_bf[1][:, half:V, 2], in_=cells[2][:, half:V])
+        nc.scalar.copy(out=z_bf[1][:, 0:half, 2:4], in_=cells[0][:, 0:half].unsqueeze(2).to_broadcast([P, half, 2]))
+        nc.scalar.copy(out=z_bf[1][:, half:V, 2], in_=cells[0][:, half:V])
         for q in (0, 1):
             cols = slice(q * BANK, (q + 1) * BANK)
-            nc.vector.tensor_copy(out=z_bf[1][:, cols, 3], in_=cells[3][:, cols])
+            nc.vector.tensor_copy(out=z_bf[1][:, cols, 3], in_=cells[1][:, cols])
         for q in (2, 3):
             cols = slice(q * BANK, (q + 1) * BANK)
-            nc.scalar.copy(out=z_bf[1][:, cols, 3], in_=cells[3][:, cols])
+            nc.scalar.copy(out=z_bf[1][:, cols, 3], in_=cells[1][:, cols])
         for q in range(4):
             z_quantize(1, q * BANK, (q + 1) * BANK)
             layer2(1, q)

@@ -19,7 +19,9 @@ P = 128
 PACK = 4
 KP = P * PACK
 BANK = 512
-X_CHUNKS = [512, 512, 512, 256, 256]
+X_CHUNKS = [512, 512, 512, 256, 128, 128]
+X_SCALAR = [0, 256, 256, 128, 128, 0]
+OUT_CHUNKS = [(0, 512), (512, 1024), (1024, 1536), (1536, 1792), (1792, 2048)]
 
 
 def tile_picked_voxel_gelu_e_kernel(tc, xT, w1, w2, gate, offs, pos1, out):
@@ -32,8 +34,8 @@ def tile_picked_voxel_gelu_e_kernel(tc, xT, w1, w2, gate, offs, pos1, out):
         pos_sb = keep.tile([P, S // 16], U16, name="pos_sb")
         x_raw = [keep.tile([P, PACK, w], F32, name="x_raw%d" % i, tag="big%d" % i, align_bytes=64) for i, w in enumerate(X_CHUNKS)]
         x_bf = [keep.tile([P, w, PACK], BF16, name="x_bf%d" % i, align_bytes=64) for i, w in enumerate(X_CHUNKS)]
-        x_codes = keep.tile([P, T], U32, name="x_codes", tag="later1", align_bytes=64)
-        x_scales = keep.tile([P, T], U8, name="x_scales", tag="later2", align_bytes=64)
+        x_codes = keep.tile([P, T], U32, name="x_codes", align_bytes=64)
+        x_scales = keep.tile([P, T], U8, name="x_scales", align_bytes=64)
         g_codes = keep.tile([P, S], U32, name="g_codes", align_bytes=64)
         g_scales = [keep.tile([P, BANK], U8, name="g_scales0", align_bytes=64)]
         w1_raw = [keep.tile([P, PACK, KP // 2], F32, name="w1_raw%d" % i, align_bytes=64) for i in range(4)]
@@ -47,13 +49,13 @@ def tile_picked_voxel_gelu_e_kernel(tc, xT, w1, w2, gate, offs, pos1, out):
         w2_scales = keep.tile([P, 2 * N], U8, name="w2_scales", align_bytes=64)
         gate_sb = keep.tile([P, S], F32, name="gate_sb", align_bytes=64)
         h_sb = {}
-        cells = [keep.tile([P, V], F32, name="cells0", align_bytes=64)]
+        cells = [keep.tile([P, V], F32, name="cells%d" % t, align_bytes=64) for t in range(3)]
         pairs = keep.tile([P, 2, V, 2], BF16, name="pairs", tag="pairs", align_bytes=64)
         z_bf = [keep.tile([P, V, PACK], BF16, name="z_bf0", align_bytes=64)]
         z_codes = keep.tile([P, 2, V], U32, name="z_codes", align_bytes=64)
         z_scales = keep.tile([P, 2, V], U8, name="z_scales", align_bytes=64)
         warm = keep.tile([P, 8], F32, name="warm")
-        out_ps = [psum.tile([P, BANK], F32, name="out_ps%d" % q) for q in range(4)]
+        out_ps = [psum.tile([P, b - a], F32, name="out_ps%d" % q) for q, (a, b) in enumerate(OUT_CHUNKS)]
 
         xv = xT.rearrange("(p j) w -> p j w", j=PACK)
         w1v = w1.rearrange("(p j) c -> p j c", j=PACK)
@@ -75,6 +77,8 @@ def tile_picked_voxel_gelu_e_kernel(tc, xT, w1, w2, gate, offs, pos1, out):
         nc.scalar.activation(out=warm[:, 4:5], in_=warm[:, 0:1], func=GELU)
         nc.vector.memset(x_scales[:].bitcast(I32), 0)
         nc.vector.memset(cells[0][:].bitcast(I32), 0)
+        for t in (1, 2):
+            nc.scalar.copy(out=cells[t][:], in_=warm[:, 0:1].to_broadcast([P, V]))
 
         def quantize(codes, scales, src):
             nc.vector.quantize_mx(out=codes.bitcast(FP8X4), scales=scales, in_=src)
@@ -83,9 +87,11 @@ def tile_picked_voxel_gelu_e_kernel(tc, xT, w1, w2, gate, offs, pos1, out):
             engine_copy(out=dst.rearrange("p (c i) t -> p c t i", i=4), in_=src.rearrange("p t (c i) -> p c t i", i=4))
 
         for i, w in enumerate(X_CHUNKS):
-            cut = w * 3 // 8
-            interleave(nc.scalar.copy, x_bf[i][:, 0:cut, :], x_raw[i][:, :, 0:cut])
-            interleave(nc.vector.tensor_copy, x_bf[i][:, cut:w, :], x_raw[i][:, :, cut:w])
+            cut = X_SCALAR[i]
+            if cut > 0:
+                interleave(nc.scalar.copy, x_bf[i][:, 0:cut, :], x_raw[i][:, :, 0:cut])
+            if cut < w:
+                interleave(nc.vector.tensor_copy, x_bf[i][:, cut:w, :], x_raw[i][:, :, cut:w])
             cols = slice(starts[i], starts[i] + w)
             quantize(x_codes[:, cols], x_scales[:, cols], x_bf[i][:].rearrange("p w t -> p (w t)"))
 
@@ -100,10 +106,6 @@ def tile_picked_voxel_gelu_e_kernel(tc, xT, w1, w2, gate, offs, pos1, out):
             cols = slice(c * KP + t0 * P, c * KP + t1 * P)
             quantize(w1_codes[:, cols], w1_scales[:, cols], w1_bf[c][:, t0:t1, :, :].rearrange("p t m j -> p (t m j)"))
 
-        def new_cells(t):
-            cells.append(keep.tile([P, V], F32, name="cells%d" % t, tag="later%d" % t, align_bytes=64))
-            nc.gpsimd.memset(cells[t][:], 0.0)
-
         def gather_codes(half):
             lst = offs_sb[:, half * 32:(half + 1) * 32]
             nc.vector.tensor_copy(g_codes[:, half * BANK:(half + 1) * BANK], x_codes[:].indirect(lst))
@@ -117,7 +119,7 @@ def tile_picked_voxel_gelu_e_kernel(tc, xT, w1, w2, gate, offs, pos1, out):
             wc = slice(n * P, (n + 1) * P)
             if half == 0:
                 h_sb.setdefault(n, keep.tile([P, S], F32, name="h_sb", bufs=5, align_bytes=64))
-            acc = psum.tile([P, BANK], F32, name="h_ps", bufs=4)
+            acc = psum.tile([P, BANK], F32, name="h_ps", bufs=3)
             nc.tensor.matmul_mx(
                 out=acc[:], lhsT=w1_codes[:, wc].bitcast(FP8X4), lhsT_scale=w1_scales[:, wc],
                 rhs=g_codes[:, cols].bitcast(FP8X4), rhs_scale=g_scales[half][:], start=True, stop=True,
@@ -125,16 +127,11 @@ def tile_picked_voxel_gelu_e_kernel(tc, xT, w1, w2, gate, offs, pos1, out):
             nc.scalar.activation(out=h_sb[n][:, cols], in_=acc[:], func=GELU)
 
         def scatter(n, a, b):
-            if n in (1, 2):
-                hg = keep.tile([P, S], F32, name="hg", bufs=2, align_bytes=64)
-                nc.vector.tensor_tensor(hg[:], h_sb[n][:], gate_sb[:], MULT)
-                nc.vector.tensor_copy(cells[n % 3][:].indirect(pos_sb[:]), hg[:])
-                return
             nc.vector.tensor_tensor(
                 cells[n % 3][:].indirect(pos_sb[:, a // 16:b // 16]), h_sb[n][:, a:b], gate_sb[:, a:b], MULT)
 
         def layer2(c, q):
-            cols = slice(q * BANK, (q + 1) * BANK)
+            cols = slice(*OUT_CHUNKS[q])
             wc = slice(c * N, (c + 1) * N)
             nc.tensor.matmul_mx(
                 out=out_ps[q][:], lhsT=w2_codes[:, wc].bitcast(FP8X4), lhsT_scale=w2_scales[:, wc],
@@ -161,8 +158,6 @@ def tile_picked_voxel_gelu_e_kernel(tc, xT, w1, w2, gate, offs, pos1, out):
         gather_scales(1)
         w1_quantize(0, 1, 2)
         w1_quantize(0, 2, 4)
-        new_cells(1)
-        new_cells(2)
         layer1(0, 0)
         layer1(0, 1)
         layer1(1, 0)
@@ -201,25 +196,25 @@ def tile_picked_voxel_gelu_e_kernel(tc, xT, w1, w2, gate, offs, pos1, out):
         nc.scalar.copy(out=z_bf[1][:, :, 1], in_=cells[2][:])
         z_quantize(0, 0, V // 2)
         z_quantize(0, V // 2, V)
-        for q in range(4):
+        for q in range(5):
             layer2(0, q)
         scatter(7, 0, S)
         half = V // 2
         nc.scalar.copy(out=z_bf[1][:, 0:half, 2:4], in_=cells[0][:, 0:half].unsqueeze(2).to_broadcast([P, half, 2]))
         nc.scalar.copy(out=z_bf[1][:, half:V, 2], in_=cells[0][:, half:V])
         for q in (0, 1):
-            cols = slice(q * BANK, (q + 1) * BANK)
+            cols = slice(*OUT_CHUNKS[q])
             nc.vector.tensor_copy(out=z_bf[1][:, cols, 3], in_=cells[1][:, cols])
-        for q in (2, 3):
-            cols = slice(q * BANK, (q + 1) * BANK)
+        for q in (2, 3, 4):
+            cols = slice(*OUT_CHUNKS[q])
             nc.scalar.copy(out=z_bf[1][:, cols, 3], in_=cells[1][:, cols])
-        for q in range(4):
-            z_quantize(1, q * BANK, (q + 1) * BANK)
+        for q in range(5):
+            z_quantize(1, *OUT_CHUNKS[q])
             layer2(1, q)
         out_sb = keep.tile([P, V], F32, name="out_sb", tag="big0", align_bytes=64)
-        for q in range(4):
-            cols = slice(q * BANK, (q + 1) * BANK)
-            if q == 2:
+        for q in range(5):
+            cols = slice(*OUT_CHUNKS[q])
+            if q >= 3:
                 nc.vector.tensor_copy(out=out_sb[:, cols], in_=out_ps[q][:])
             else:
                 nc.scalar.copy(out=out_sb[:, cols], in_=out_ps[q][:])

from contextlib import ExitStack

import concourse.mybir as mybir

K, T, S, V, H, N = 512, 2048, 1024, 2048, 1024, 128
FLOPS = 2 * K * H * S + 2 * H * N * V

F32 = mybir.dt.float32
BF16 = mybir.dt.bfloat16
I32 = mybir.dt.int32
U32 = mybir.dt.uint32
U16 = mybir.dt.uint16
U8 = mybir.dt.uint8
FP8X4 = mybir.dt.float8_e4m3fn_x4
GELU = mybir.ActivationFunctionType.Gelu_apprx_tanh
MULT = mybir.AluOpType.mult

P = 128
PACK = 4
KP = P * PACK
BANK = 512
X_CHUNKS = [512, 512, 512, 256, 128, 128]
X_SCALAR = [0, 256, 256, 128, 128, 0]
OUT_CHUNKS = [(0, 512), (512, 1024), (1024, 1536), (1536, 1792), (1792, 2048)]


def tile_picked_voxel_gelu_e_kernel(tc, xT, w1, w2, gate, offs, pos1, out):
    nc = tc.nc
    with ExitStack() as ctx:
        keep = ctx.enter_context(tc.tile_pool(name="keep", bufs=1))
        psum = ctx.enter_context(tc.psum_pool(name="psum", bufs=1))

        offs_sb = keep.tile([P, S // 16], U16, name="offs_sb")
        pos_sb = keep.tile([P, S // 16], U16, name="pos_sb")
        x_raw = [keep.tile([P, PACK, w], F32, name="x_raw%d" % i, tag="big%d" % i, align_bytes=64) for i, w in enumerate(X_CHUNKS)]
        x_bf = [keep.tile([P, w, PACK], BF16, name="x_bf%d" % i, align_bytes=64) for i, w in enumerate(X_CHUNKS)]
        x_codes = keep.tile([P, T], U32, name="x_codes", align_bytes=64)
        x_scales = keep.tile([P, T], U8, name="x_scales", align_bytes=64)
        g_codes = keep.tile([P, S], U32, name="g_codes", align_bytes=64)
        g_scales = [keep.tile([P, BANK], U8, name="g_scales0", align_bytes=64)]
        w1_raw = [keep.tile([P, PACK, KP // 2], F32, name="w1_raw%d" % i, align_bytes=64) for i in range(4)]
        w1_first = keep.tile([P, P, PACK], BF16, name="w1_first", tag="later0", align_bytes=64)
        w1_bf = [keep.tile([P, PACK, P, PACK], BF16, name="w1_bf%d" % c, align_bytes=64) for c in range(2)]
        w1_codes = keep.tile([P, H], U32, name="w1_codes", align_bytes=64)
        w1_scales = keep.tile([P, H], U8, name="w1_scales", align_bytes=64)
        w2_raw = keep.tile([P, 2, PACK, N], F32, name="w2_raw", align_bytes=64)
        w2_bf = keep.tile([P, 2, N, PACK], BF16, name="w2_bf", align_bytes=64)
        w2_codes = keep.tile([P, 2 * N], U32, name="w2_codes", align_bytes=64)
        w2_scales = keep.tile([P, 2 * N], U8, name="w2_scales", align_bytes=64)
        gate_sb = keep.tile([P, S], F32, name="gate_sb", align_bytes=64)
        h_sb = {}
        cells = [keep.tile([P, V], F32, name="cells%d" % t, align_bytes=64) for t in range(3)]
        pairs = keep.tile([P, 2, V, 2], BF16, name="pairs", tag="pairs", align_bytes=64)
        z_bf = [keep.tile([P, V, PACK], BF16, name="z_bf0", align_bytes=64)]
        z_codes = keep.tile([P, 2, V], U32, name="z_codes", align_bytes=64)
        z_scales = keep.tile([P, 2, V], U8, name="z_scales", align_bytes=64)
        warm = keep.tile([P, 8], F32, name="warm")
        out_ps = [psum.tile([P, b - a], F32, name="out_ps%d" % q) for q, (a, b) in enumerate(OUT_CHUNKS)]

        xv = xT.rearrange("(p j) w -> p j w", j=PACK)
        w1v = w1.rearrange("(p j) c -> p j c", j=PACK)
        starts = [sum(X_CHUNKS[:i]) for i in range(len(X_CHUNKS))]
        for i, w in enumerate(X_CHUNKS):
            if i == len(X_CHUNKS) - 1:
                nc.sync.dma_start(offs_sb[:], offs)
            nc.sync.dma_start(out=x_raw[i][:], in_=xv[:, :, starts[i]:starts[i] + w])
        for i in range(2):
            nc.sync.dma_start(out=w1_raw[i][:], in_=w1v[:, :, i * 256:(i + 1) * 256])
        nc.sync.dma_start(pos_sb[:], pos1)
        nc.sync.dma_start(out=gate_sb[:], in_=gate)
        for i in range(2, 4):
            nc.sync.dma_start(out=w1_raw[i][:], in_=w1v[:, :, i * 256:(i + 1) * 256])
        for c in range(2):
            nc.sync.dma_start(out=w2_raw[:, c, :, :], in_=w2[c * KP:(c + 1) * KP, :].rearrange("(p j) n -> p j n", j=PACK))

        nc.vector.memset(warm[:, 0:1], 0.0)
        nc.scalar.activation(out=warm[:, 4:5], in_=warm[:, 0:1], func=GELU)
        nc.vector.memset(x_scales[:].bitcast(I32), 0)
        nc.vector.memset(cells[0][:].bitcast(I32), 0)
        for t in (1, 2):
            nc.scalar.copy(out=cells[t][:], in_=warm[:, 0:1].to_broadcast([P, V]))

        def quantize(codes, scales, src):
            nc.vector.quantize_mx(out=codes.bitcast(FP8X4), scales=scales, in_=src)

        def interleave(engine_copy, dst, src):
            engine_copy(out=dst.rearrange("p (c i) t -> p c t i", i=4), in_=src.rearrange("p t (c i) -> p c t i", i=4))

        for i, w in enumerate(X_CHUNKS):
            cut = X_SCALAR[i]
            if cut > 0:
                interleave(nc.scalar.copy, x_bf[i][:, 0:cut, :], x_raw[i][:, :, 0:cut])
            if cut < w:
                interleave(nc.vector.tensor_copy, x_bf[i][:, cut:w, :], x_raw[i][:, :, cut:w])
            cols = slice(starts[i], starts[i] + w)
            quantize(x_codes[:, cols], x_scales[:, cols], x_bf[i][:].rearrange("p w t -> p (w t)"))

        def w1_copy(c, t0):
            for half in range(2):
                nc.scalar.copy(
                    out=w1_bf[c][:, t0:PACK, half * 64:(half + 1) * 64, :].rearrange("p t m j -> p m j t"),
                    in_=w1_raw[2 * c + half][:].rearrange("p j (m t) -> p m j t", t=PACK)[:, :, :, t0:PACK],
                )

        def w1_quantize(c, t0, t1):
            cols = slice(c * KP + t0 * P, c * KP + t1 * P)
            quantize(w1_codes[:, cols], w1_scales[:, cols], w1_bf[c][:, t0:t1, :, :].rearrange("p t m j -> p (t m j)"))

        def gather_codes(half):
            lst = offs_sb[:, half * 32:(half + 1) * 32]
            nc.vector.tensor_copy(g_codes[:, half * BANK:(half + 1) * BANK], x_codes[:].indirect(lst))

        def gather_scales(half):
            lst = offs_sb[:, half * 32:(half + 1) * 32]
            nc.vector.tensor_copy(g_scales[half][:], x_scales[:].indirect(lst))

        def layer1(n, half):
            cols = slice(half * BANK, (half + 1) * BANK)
            wc = slice(n * P, (n + 1) * P)
            if half == 0:
                h_sb.setdefault(n, keep.tile([P, S], F32, name="h_sb", bufs=5, align_bytes=64))
            acc = psum.tile([P, BANK], F32, name="h_ps", bufs=3)
            nc.tensor.matmul_mx(
                out=acc[:], lhsT=w1_codes[:, wc].bitcast(FP8X4), lhsT_scale=w1_scales[:, wc],
                rhs=g_codes[:, cols].bitcast(FP8X4), rhs_scale=g_scales[half][:], start=True, stop=True,
            )
            nc.scalar.activation(out=h_sb[n][:, cols], in_=acc[:], func=GELU)

        def scatter(n, a, b):
            nc.vector.tensor_tensor(
                cells[n % 3][:].indirect(pos_sb[:, a // 16:b // 16]), h_sb[n][:, a:b], gate_sb[:, a:b], MULT)

        def layer2(c, q):
            cols = slice(*OUT_CHUNKS[q])
            wc = slice(c * N, (c + 1) * N)
            nc.tensor.matmul_mx(
                out=out_ps[q][:], lhsT=w2_codes[:, wc].bitcast(FP8X4), lhsT_scale=w2_scales[:, wc],
                rhs=z_codes[:, c, cols].bitcast(FP8X4), rhs_scale=z_scales[:, c, cols], start=(c == 0), stop=(c == 1),
            )

        def z_quantize(c, a, b):
            quantize(z_codes[:, c, a:b], z_scales[:, c, a:b], z_bf[c][:, a:b, :].rearrange("p v t -> p (v t)"))

        def to_pairs(t):
            nc.scalar.copy(out=pairs[:, t // 2, :, t % 2], in_=cells[t % 3][:])

        for half in range(2):
            nc.scalar.copy(
                out=w1_first[:, half * 64:(half + 1) * 64, :],
                in_=w1_raw[half][:].rearrange("p j (m t) -> p t m j", t=PACK)[:, 0, :, :],
            )
        w1_copy(0, 1)
        gather_codes(0)
        gather_scales(0)
        gather_codes(1)
        quantize(w1_codes[:, 0:P], w1_scales[:, 0:P], w1_first[:].rearrange("p m j -> p (m j)"))
        g_scales.append(keep.tile([P, BANK], U8, name="g_scales1", tag="later0", align_bytes=64))
        gather_scales(1)
        w1_quantize(0, 1, 2)
        w1_quantize(0, 2, 4)
        layer1(0, 0)
        layer1(0, 1)
        layer1(1, 0)
        layer1(1, 1)
        w1_copy(1, 0)
        scatter(0, 0, BANK)
        scatter(0, BANK, S)
        w1_quantize(1, 0, 4)
        for n in (2, 3):
            layer1(n, 0)
            layer1(n, 1)
        scatter(1, 0, S)
        to_pairs(0)
        for c in range(2):
            interleave(nc.scalar.copy, w2_bf[:, c, :, :], w2_raw[:, c, :, :])
        for n in (4, 5):
            layer1(n, 0)
            layer1(n, 1)
        scatter(2, 0, S)
        to_pairs(1)
        for n in (6, 7):
            layer1(n, 0)
            layer1(n, 1)
        scatter(3, 0, S)
        quantize(w2_codes[:], w2_scales[:], w2_bf[:].rearrange("p c n j -> p (c n j)"))
        to_pairs(2)
        scatter(4, 0, S)
        to_pairs(3)
        words = pairs[:].rearrange("p u v e -> p u (v e)").bitcast(F32)
        z0_words = z_bf[0][:].rearrange("p v t -> p (v t)").bitcast(F32).rearrange("p (v u) -> p v u", u=2)
        interleave(nc.scalar.copy, z0_words, words)
        z_bf.append(keep.tile([P, V, PACK], BF16, name="z_bf1", tag="pairs", align_bytes=64))
        scatter(5, 0, S)
        nc.scalar.copy(out=z_bf[1][:, :, 0], in_=cells[1][:])
        scatter(6, 0, S)
        nc.scalar.copy(out=z_bf[1][:, :, 1], in_=cells[2][:])
        z_quantize(0, 0, V // 2)
        z_quantize(0, V // 2, V)
        for q in range(5):
            layer2(0, q)
        scatter(7, 0, S)
        half = V // 2
        nc.scalar.copy(out=z_bf[1][:, 0:half, 2:4], in_=cells[0][:, 0:half].unsqueeze(2).to_broadcast([P, half, 2]))
        nc.scalar.copy(out=z_bf[1][:, half:V, 2], in_=cells[0][:, half:V])
        for q in (0, 1):
            cols = slice(*OUT_CHUNKS[q])
            nc.vector.tensor_copy(out=z_bf[1][:, cols, 3], in_=cells[1][:, cols])
        for q in (2, 3, 4):
            cols = slice(*OUT_CHUNKS[q])
            nc.scalar.copy(out=z_bf[1][:, cols, 3], in_=cells[1][:, cols])
        for q in range(5):
            z_quantize(1, *OUT_CHUNKS[q])
            layer2(1, q)
        out_sb = keep.tile([P, V], F32, name="out_sb", tag="big0", align_bytes=64)
        for q in range(5):
            cols = slice(*OUT_CHUNKS[q])
            if q >= 3:
                nc.vector.tensor_copy(out=out_sb[:, cols], in_=out_ps[q][:])
            else:
                nc.scalar.copy(out=out_sb[:, cols], in_=out_ps[q][:])
            nc.sync.dma_start(out=out[:, cols], in_=out_sb[:, cols])
